import numpy as np, ml_dtypes
CORES = [3,7,11,15,131,135,139,143]
N = 8
import mx_ref
BF = ml_dtypes.bfloat16
def entries(a):
    return np.ascontiguousarray(a.T).reshape(-1)
def table(e):
    return np.ascontiguousarray(np.reshape(e, (-1, 16)).T).astype(np.int32)
def cols(t, e):
    v = np.concatenate([t.reshape(128, -1, 4), np.zeros((128, 1, 4), BF)], axis=1)
    return np.ascontiguousarray(v[:, e]).reshape(128, -1)
def f(rng, *shape):
    return mx_ref.flush((rng.standard_normal(shape, dtype=np.float32) * np.exp2(rng.integers(-2, 3, shape[:-1] + (1,)))).astype(BF))
def wide(rng, *shape, cols=0):
    v = rng.standard_normal(shape, dtype=np.float32) * np.exp2(rng.integers(-12, 13, shape)).astype(np.float32)
    if cols: v *= np.repeat(np.exp2(rng.integers(-cols, cols + 1, shape[:-2] + (1, shape[-1] // 4))) * (rng.random(shape[:-2] + (1, shape[-1] // 4)) > 0.0625), 4, axis=-1).astype(np.float32)
    return mx_ref.flush(v.astype(BF))
TA, TB, CI, CJ, JW = 256, 256, 24, 64, 384
SIDE = [0 if c < 128 else 1 for c in CORES]
GCOL = [SIDE[:r].count(SIDE[r]) for r in range(N)]
def fill(rng, total, cap, wd, first, back):
    n = np.zeros(N, int)
    for q in first: n[q] = min(cap, total - n.sum())
    while n.sum() < total:
        q = rng.integers(0, N)
        if n[q] < cap: n[q] += 1
    s, used = np.full((N, cap), -1), []
    for q in range(N):
        k, v = rng.permutation(cap)[:n[q]], rng.integers(0, wd, n[q])
        if back: k, v = np.sort(k), np.sort(v)[::-1]
        s[q, k] = v; used += list(q * cap + k)
    return s, (np.sort(used)[::-1] if back else rng.permutation(used))
def lists(rng, full=False, own=False, back=False, alike=False):
    A, B = [], []
    for i in range(2):
        A.append(fill(rng, 128, CI, TA, rng.permutation(N) if full else [r for r in range(N) if own and SIDE[r] == i], back))
    for k in range(4):
        B.append(fill(rng, JW, CJ, TB, rng.permutation(N) if full else [r for r in range(N) if own and GCOL[r] == k], back))
    if alike: B = [B[0]] * 4
    return {"sa": np.stack([table(np.concatenate([A[i][0][q] for i in range(2)])) for q in range(N)]),
            "sb": np.stack([table(np.concatenate([B[k][0][q] for k in range(4)])) for q in range(N)]),
            "pi": np.stack([table(A[SIDE[r]][1]) for r in range(N)]), "pj": np.stack([table(B[GCOL[r]][1]) for r in range(N)])}
def setup_inputs(rng):
    return {"a": f(rng, N, 128, 4 * TA), "b": f(rng, N, 128, 4 * TB), **lists(rng)}
def setup_inputs_alike(rng):
    return {**setup_inputs(rng), **lists(rng, alike=True)}
def setup_inputs_full(rng):
    return {**setup_inputs(rng), **lists(rng, full=True)}
def setup_inputs_own(rng):
    return {**setup_inputs(rng), **lists(rng, own=True)}
def setup_inputs_reversed(rng):
    return {**setup_inputs(rng), **lists(rng, back=True)}
def setup_inputs_spread(rng):
    d = setup_inputs(rng); d["a"], d["b"] = wide(rng, N, 128, 4 * TA, cols=6), wide(rng, N, 128, 4 * TB, cols=6); return d
def check_inputs(d):
    bad = []
    for s, p, wd, cap, total, place in (("sa", "pi", TA, CI, 128, SIDE), ("sb", "pj", TB, CJ, JW, GCOL)):
        e = np.stack([entries(d[s][q]) for q in range(N)])
        if e.min() < -1 or e.max() >= wd: bad.append(s)
        for r in range(N):
            v = e[:, cap * place[r]:cap * place[r] + cap].reshape(-1)
            if (v >= 0).sum() != total: bad.append(s + " count")
            t = entries(d[p][r])
            if t.min() < 0 or t.max() >= N * cap: bad.append(p); continue
            if len(set(t.tolist())) != total or (v[t] < 0).any(): bad.append(p + " slots")
            if (d[p][r] != d[p][place.index(place[r])]).any(): bad.append(p + " not the same")
    return bad
def reference(a, b, sa, sb, pi, pj):
    y = np.zeros((N, 128, JW), np.float32)
    for r in range(N):
        i, k = SIDE[r], GCOL[r]
        A = np.concatenate([cols(a[q], entries(sa[q])[CI * i:CI * i + CI]) for q in range(N)], axis=1)
        B = np.concatenate([cols(b[q], entries(sb[q])[CJ * k:CJ * k + CJ]) for q in range(N)], axis=1)
        y[r] = mx_ref.matmul(mx_ref.quantize(cols(A, entries(pi[r]))), mx_ref.quantize(cols(B, entries(pj[r]))))
    return {"y": y}

from concourse.bass import DstId, RemoteDMATransfer, IndirectOffsetOnAxis
from concourse.mybir import dt, AluOpType, AxisListType, ActivationFunctionType

N, CI, CJ, JW = 8, 24, 64, 384
CODES = "float8_e4m3fn_x4"
RELAY, NEIGH, DIRECT, OWN, AEND = 0, 72, 96, 168, 200
SET1 = 72
MISS = 1000

SCRATCH = {
    "aw": ("sbuf", [128, 1032], "bfloat16"), "bw": ("sbuf", [128, 1032], "bfloat16"),
    "ha": ("sbuf", [128, 512], "bfloat16"), "hb": ("sbuf", [128, 1024], "bfloat16"),
    "qa": ("sbuf", [128, 128], CODES), "za": ("sbuf", [128, 128], "uint8"),
    "qb": ("sbuf", [128, 256], CODES), "zb": ("sbuf", [128, 256], "uint8"),
    "ac": ("sbuf", [128, AEND], CODES), "az": ("sbuf", [128, AEND], "uint8"),
    "bc": ("sbuf", [128, 512], CODES), "bz": ("sbuf", [128, 512], "uint8"),
    "la": ("sbuf", [128, 3], "int32"), "lb": ("sbuf", [128, 16], "int32"),
    "lp": ("sbuf", [128, 8], "int32"), "lj": ("sbuf", [128, 24], "int32"),
    "oa": ("sbuf", [128, 16], "uint16"), "ob": ("sbuf", [128, 64], "uint16"),
    "opi": ("sbuf", [128, 8], "uint16"), "opj": ("sbuf", [128, 24], "uint16"),
    "ip": ("sbuf", [128, 1], "int32"), "ix": ("sbuf", [128, 1], "int32"),
    "cc": ("sbuf", [128, AEND], "float32"),
    "pf": ("sbuf", [128, 1], "float32"), "pg": ("sbuf", [128, 1], "float32"),
    "iw": ("sbuf", [128, N * CI], "float32"), "il": ("sbuf", [128, AEND], "float32"),
    "m1": ("sbuf", [128, 128], "float32"), "m2": ("sbuf", [128, SET1], "float32"),
    "t1": ("sbuf", [128, 128], "float32"), "t2": ("sbuf", [128, SET1], "float32"),
    "r1": ("sbuf", [128, 1], "float32"), "r2": ("sbuf", [128, 1], "float32"),
    "x1": ("sbuf", [128, 1], "int32"), "x2": ("sbuf", [128, 1], "int32"),
    "z1": ("sbuf", [128, 512], "float32"), "z2": ("sbuf", [128, 512], "float32"),
    "y1": ("sbuf", [128, JW], "float32"), "y2": ("sbuf", [128, JW], "float32"),
    "p1": ("psum", [128, 2048], "float32"), "p2": ("psum", [128, 1024], "float32"),
}
SEMAPHORES = (["d_a", "d_b", "d_sa", "d_sb", "d_pi", "d_owa", "d_owb",
               "k_pj", "k_y",
               "g_p", "g_c", "v_z", "v_ix", "v_oa", "v_ob", "v_ga", "v_gb", "s_ga", "s_gb", "v_qa", "v_qb",
               "v_w", "v_oj", "v_idx", "v_c1", "s_c1", "v_c2", "s_c2", "v_y1", "s_y1", "v_y2", "s_y2",
               "m_20", "m_21", "left", "r_an", "r_ad", "r_ar"]
              + ["m_1%d" % n for n in range(4)] + ["r_b%d" % n for n in range(4)])


def places(T, topo):
    cores = list(T.cores)
    host0 = topo.host(cores[0])
    side = [0 if topo.host(c) == host0 else 1 for c in cores]
    gcol = [side[:r].count(side[r]) for r in range(N)]
    nb = [[q for q in range(N) if q != r and cores[q] in topo.cores_of(cores[r])][0] for r in range(N)]
    direct = [[q for q in range(N) if q != r and topo.die(cores[q]) == topo.die(cores[r])] for r in range(N)]
    return cores, side, gcol, nb, direct


def plan(r, T, topo):
    cores, side, gcol, nb, direct = places(T, topo)
    c, n = cores[r], nb[r]
    off = topo.engines(c, cores[direct[r][0]])
    near = [e for e in topo.engines(c, cores[n]) if e not in off][:4]
    h = len(off) // 2
    lo, hi = off[:h], off[h:]
    others = [q for q in range(N) if q not in (r, n)]

    def far(q):
        return side[q] != side[r] and not topo.same_plane(c, cores[q])

    def apiece(q, eng, codes):
        at = NEIGH if q == n else DIRECT + CI * direct[q].index(r)
        return (q, eng, "r_an" if q == n else "r_ad", "qa" if codes else "za", 8 + CI * side[q], "ac" if codes else "az", at, CI)

    def bpiece(q, eng, codes):
        return (q, eng, "r_b%d" % (r // 2), "qb" if codes else "zb", CJ * gcol[q], "bc" if codes else "bz", CJ * r, CJ)

    f3 = [q for q in direct[r] if far(q)][0]
    o3 = [q for q in direct[r] if q != f3]
    f2 = [q for q in others if far(q)]
    mate = [q for q in others if side[q] == side[r]]
    same = [q for q in others if q not in f2 and q not in mate]
    a1 = [apiece(f3, lo, 1), apiece(o3[0], hi[:2], 1), apiece(o3[1], hi[2:], 1), apiece(n, near, 1)]
    a2 = [apiece(o3[0], hi, 0), apiece(f3, lo[:2], 0), apiece(o3[1], lo[2:], 0), apiece(n, near, 0)]
    b1 = [bpiece(f2[0], lo[:2], 1), bpiece(f2[1], lo[2:], 1)] + [bpiece(q, hi[x:x + 1], 1) for x, q in enumerate(mate + same)] + [bpiece(n, near, 1)]
    b2 = [bpiece(same[0], hi[:2], 0), bpiece(same[1], hi[2:], 0)] + [bpiece(q, lo[x:x + 1], 0) for x, q in enumerate(f2 + mate)] + [bpiece(n, near, 0)]
    f1 = [(n, near, "r_ar", "ac", DIRECT, "ac", RELAY, 3 * CI)]
    f2_ = [(n, near, "r_ar", "az", DIRECT, "az", RELAY, 3 * CI)]
    return [a1, a2, b1, b2, f1, f2_]


def view(t, a, n):
    v = t[:, a:a + n]
    return v.bitcast(dt.uint8) if t.dtype != dt.uint8 else v


def rank_program(g, core, T, topo):
    rank = T.rank_of(core)
    if rank is None:
        return
    S = T.sem
    cores, side, gcol, nb, direct = places(T, topo)
    calls = plan(rank, T, topo)
    due = {}
    for q in range(N):
        if q != rank:
            for call in plan(q, T, topo):
                for w in call:
                    if w[0] == rank:
                        due[w[2]] = due.get(w[2], 0) + len(w[1])
    left = sum(len(w[1]) for call in calls for w in call)
    V, A, P, Y = g.vector, g.scalar, g.tensor, g.sync
    COPY = ActivationFunctionType.Copy
    own = rank // 2
    me = side[rank]

    def send(call):
        out = []
        for q, eng, sem, sb, sa, db, da, n in call:
            rid, pid = topo.addr(cores[q], core)
            out.append(RemoteDMATransfer(dst_ids=[DstId(rid=rid, pnc=pid)], dma_engine_mask=sum(1 << e for e in eng),
                                         remote_sem=S[sem], src=view(T[sb], sa, n), dst=view(T[db], da, n)))
        g.remote_dma_fused(out, local_sem=S.left)

    def rankof(n):
        c = cores[2 * n]
        return 0 if n == own else 1 if side[2 * n] == me else 2 if topo.same_plane(core, c) else 3
    order = sorted(range(4), key=rankof)

    for k in range(4, 8):
        A.dma_start(T.la[16 * k:16 * k + 16, :], T.sa[:, :]).then_inc(S.d_sa, 16)
    for k in range(4, 8):
        A.dma_start(T.lb[16 * k:16 * k + 16, :], T.sb[:, :]).then_inc(S.d_sb, 16)
    A.dma_start(T.bw[:, 8:1032], T.b[:, :]).then_inc(S.d_b, 16)

    for k in range(4):
        Y.dma_start(T.la[16 * k:16 * k + 16, :], T.sa[:, :]).then_inc(S.d_sa, 16)
    Y.dma_start(T.aw[:, 8:1032], T.a[:, :]).then_inc(S.d_a, 16)
    for k in range(4):
        Y.dma_start(T.lb[16 * k:16 * k + 16, :], T.sb[:, :]).then_inc(S.d_sb, 16)
    for k in range(8):
        Y.dma_start(T.lp[16 * k:16 * k + 16, :], T.pi[:, :]).then_inc(S.d_pi, 16)
    o0 = 0 if me == 0 else 32
    Y.wait_ge(S.v_qa, 1)
    Y.dma_start(view(T.ac, OWN, 32), view(T.qa, o0, 32)).then_inc(S.d_owa, 16)
    Y.dma_start(view(T.az, OWN, 32), view(T.za, o0, 32)).then_inc(S.d_owa, 16)
    Y.wait_ge(S.v_qb, 1)
    Y.dma_start(view(T.bc, CJ * rank, CJ), view(T.qb, CJ * gcol[rank], CJ)).then_inc(S.d_owb, 16)
    Y.dma_start(view(T.bz, CJ * rank, CJ), view(T.zb, CJ * gcol[rank], CJ)).then_inc(S.d_owb, 16)

    g.iota(T.ip[:, :], [[0, 1]], 0, 1).then_inc(S.g_p, 1)
    g.iota(T.cc[:, :], [[1, AEND]], 0, 0, allow_small_or_imprecise_dtypes=True).then_inc(S.g_c, 1)
    g.wait_ge(S.v_ix, 1)
    g.indirect_dma_start(T.lj[:, :], None, T.pj[:, :], IndirectOffsetOnAxis(ap=T.ix[:, 0:1], axis=0), bounds_check=15).then_inc(S.k_pj, 16)

    V.memset(T.aw[:, 0:8], 0.0).then_inc(S.v_z, 1)
    V.memset(T.bw[:, 0:8], 0.0).then_inc(S.v_z, 1)
    V.memset(T.ha[:, 0:32], 0.0).then_inc(S.v_z, 1)
    V.memset(T.ha[:, 224:512], 0.0).then_inc(S.v_z, 1)
    V.memset(T.iw[:, :], float(MISS)).then_inc(S.v_z, 1)
    V.memset(T.il[:, OWN:AEND], float(MISS)).then_inc(S.v_z, 1)
    V.wait_ge(S.g_p, 1)
    V.tensor_scalar(T.ix[:, :], T.ip[:, :], 15, None, AluOpType.bitwise_and).then_inc(S.v_ix, 1)
    V.wait_ge(S.d_sa, 128)
    for t in range(4):
        V.tensor_scalar(T.oa[:, 4 * t:4 * t + 3], T.la[:, :], 4.0, float(8 + t), AluOpType.mult, AluOpType.add).then_inc(S.v_oa, 1)
    for q, sem in ((A, S.s_ga), (V, S.v_ga)):
        q.wait_ge(S.v_z, 6)
        q.wait_ge(S.v_oa, 4)
        q.wait_ge(S.d_a, 16)
        for t in ((0, 1) if q is A else (2, 3)):
            o, i = T.ha[:, 32 + t:224:4], T.aw[:, 0:1032].indirect(T.oa[:, 4 * t:4 * t + 3])
            (q.activation(o, i, COPY) if q is A else q.tensor_copy(o, i)).then_inc(sem, 1)
    V.wait_ge(S.v_ga, 2)
    V.wait_ge(S.s_ga, 2)
    V.quantize_mx(T.qa[:, :], T.za[:, :], T.ha[:, :]).then_inc(S.v_qa, 1)
    V.wait_ge(S.d_sb, 128)
    for t in range(4):
        V.tensor_scalar(T.ob[:, 16 * t:16 * t + 16], T.lb[:, :], 4.0, float(8 + t), AluOpType.mult, AluOpType.add).then_inc(S.v_ob, 1)
    for q, sem in ((A, S.s_gb), (V, S.v_gb)):
        q.wait_ge(S.v_ob, 4)
        q.wait_ge(S.d_b, 16)
        for t in ((0, 1) if q is A else (2, 3)):
            o, i = T.hb[:, t:1024:4], T.bw[:, 0:1032].indirect(T.ob[:, 16 * t:16 * t + 16])
            (q.activation(o, i, COPY) if q is A else q.tensor_copy(o, i)).then_inc(sem, 1)
    V.wait_ge(S.v_gb, 2)
    V.wait_ge(S.s_gb, 2)
    V.quantize_mx(T.qb[:, :], T.zb[:, :], T.hb[:, :]).then_inc(S.v_qb, 1)

    g.wait_ge(S.v_qa, 1)
    send(calls[0])
    send(calls[1])
    g.wait_ge(S.v_qb, 1)
    send(calls[2])
    send(calls[3])
    g.wait_ge(S.r_ad, due["r_ad"])
    send(calls[4])
    send(calls[5])

    V.wait_ge(S.k_pj, 16)
    V.tensor_copy(T.opj[:, :], T.lj[:, :]).then_inc(S.v_oj, 1)
    w = [0]

    def chain(inst):
        inst.then_inc(S.v_w, 1)
        w[0] += 1

    V.wait_ge(S.g_c, 1)
    V.wait_ge(S.d_pi, 128)
    chain(V.tensor_copy(T.opi[:, :], T.lp[:, :]))
    chain(V.tensor_copy(T.pf[:, :], T.ip[:, :]))
    V.wait_ge(S.v_w, w[0])
    chain(V.tensor_copy(T.iw[:, :].indirect(T.opi[:, :]), T.cc[:, 0:128]))
    chain(V.tensor_scalar(T.pg[:, :], T.pf[:, :], float(SET1), None, AluOpType.add))
    V.wait_ge(S.v_w, w[0])
    n = nb[rank]
    land = [(RELAY + CI * x, q) for x, q in enumerate(direct[n])] + [(NEIGH, n)]
    land += [(DIRECT + CI * x, q) for x, q in enumerate(direct[rank])] + [(OWN + (8 if me == 0 else 0), rank)]
    for at, q in land:
        chain(V.tensor_copy(T.il[:, at:at + CI], T.iw[:, CI * q:CI * q + CI]))
    chain(V.tensor_scalar(T.m1[:, :], T.cc[:, SET1:AEND], T.pg[:, 0:1], None, AluOpType.is_equal))
    chain(V.tensor_scalar(T.m2[:, :], T.cc[:, 0:SET1], T.pf[:, 0:1], None, AluOpType.is_equal))
    V.wait_ge(S.v_w, w[0])
    chain(V.tensor_tensor(T.t1[:, :], T.m1[:, :], T.il[:, SET1:AEND], AluOpType.mult))
    chain(V.tensor_tensor(T.t2[:, :], T.m2[:, :], T.il[:, 0:SET1], AluOpType.mult))
    V.wait_ge(S.v_w, w[0])
    chain(V.tensor_reduce(T.r1[:, :], T.t1[:, :], AxisListType.X, AluOpType.add))
    chain(V.tensor_reduce(T.r2[:, :], T.t2[:, :], AxisListType.X, AluOpType.add))
    V.wait_ge(S.v_w, w[0])
    V.tensor_copy(T.x1[:, :], T.r1[:, :]).then_inc(S.v_idx, 1)
    V.tensor_copy(T.x2[:, :], T.r2[:, :]).then_inc(S.v_idx, 1)

    P.wait_ge(S.d_owa, 32)
    P.wait_ge(S.r_an, due["r_an"])
    P.wait_ge(S.r_ad, due["r_ad"])
    P.wait_ge(S.d_owb, 32)
    for x, c in enumerate(order):
        P.wait_ge(S["r_b%d" % c], due["r_b%d" % c])
        P.matmul_mx(T.p1[:, 512 * x:512 * x + 128], T.ac[:, SET1:AEND], T.az[:, SET1:AEND],
                    T.bc[:, 128 * c:128 * c + 128], T.bz[:, 128 * c:128 * c + 128], True, True).then_inc(S["m_1%d" % x], 1)
    P.wait_ge(S.r_ar, due["r_ar"])
    for x in range(2):
        P.matmul_mx(T.p2[:, 512 * x:512 * x + 256], T.ac[:, 0:128], T.az[:, 0:128],
                    T.bc[:, 256 * x:256 * x + 256], T.bz[:, 256 * x:256 * x + 256], True, True).then_inc(S["m_2%d" % x], 1)

    def copy(q, o, i, sem):
        (q.activation(o, i, COPY) if q is A else q.tensor_copy(o, i)).then_inc(sem, 1)

    A.wait_ge(S.v_oj, 1)
    V.wait_ge(S.v_oj, 1)
    for q, sem, xs in ((V, S.v_c1, (0, 2)), (A, S.s_c1, (1, 3))):
        for x in xs:
            c = order[x]
            q.wait_ge(S["m_1%d" % x], 1)
            copy(q, T.z1[:, 128 * c:128 * c + 128], T.p1[:, 512 * x:512 * x + 128], sem)
    for q, sem, j in ((V, S.v_y1, 0), (A, S.s_y1, 12)):
        q.wait_ge(S.v_c1, 2)
        q.wait_ge(S.s_c1, 2)
        copy(q, T.y1[:, 16 * j:16 * j + 192], T.z1[:, 0:512].indirect(T.opj[:, j:j + 12]), sem)
    for q, sem, x in ((V, S.v_c2, 0), (A, S.s_c2, 1)):
        q.wait_ge(S["m_2%d" % x], 1)
        copy(q, T.z2[:, 256 * x:256 * x + 256], T.p2[:, 512 * x:512 * x + 256], sem)
    for q, sem, j in ((V, S.v_y2, 0), (A, S.s_y2, 12)):
        q.wait_ge(S.v_c2, 1)
        q.wait_ge(S.s_c2, 1)
        copy(q, T.y2[:, 16 * j:16 * j + 192], T.z2[:, 0:512].indirect(T.opj[:, j:j + 12]), sem)

    g.wait_ge(S.v_idx, 2)
    g.wait_ge(S.v_y1, 1)
    g.wait_ge(S.s_y1, 1)
    g.indirect_dma_start(T.y[:, :], IndirectOffsetOnAxis(ap=T.x1[:, 0:1], axis=0), T.y1[:, :], None, bounds_check=127, oob_is_err=False).then_inc(S.k_y, 16)
    g.wait_ge(S.v_y2, 1)
    g.wait_ge(S.s_y2, 1)
    g.indirect_dma_start(T.y[:, :], IndirectOffsetOnAxis(ap=T.x2[0:SET1, 0:1], axis=0), T.y2[0:SET1, :], None, bounds_check=127, oob_is_err=False).then_inc(S.k_y, 16)
    g.wait_ge(S.left, left)
    g.wait_ge(S.k_y, 32)
